import numpy as np
import ml_dtypes


def mxq(x, axis, fmt="e4m3"):
    dtype, down = {"e4m3": (ml_dtypes.float8_e4m3fn, 7), "e5m2": (ml_dtypes.float8_e5m2, 14)}[fmt]
    v = np.moveaxis(np.asarray(x, np.float32).astype(ml_dtypes.bfloat16).astype(np.float64), axis, -1)
    blocks = v.reshape(v.shape[:-1] + (-1, 32))
    amax = np.abs(blocks).max(-1, keepdims=True)
    byte = np.maximum(np.where(amax > 0, np.frexp(amax)[1] - 1 + 127, 0) - down, 1)
    scale = np.exp2(byte - 127.0)
    codes = (blocks / scale).astype(np.float32).astype(dtype).astype(np.float64)
    return np.moveaxis((codes * scale).reshape(v.shape), -1, axis)


WIDE = False


def mx_kscale(k):
    if not WIDE:
        return np.ones(k)
    levels = np.array([10, -10, 5, -5, 0])
    if k % 512:
        return np.exp2(np.random.permutation(np.resize(levels, k // 32))).repeat(32)
    a = np.empty((k // 512, 16))
    for p in range(k // 512):
        a[p, :8] = np.random.permutation(np.resize(levels, 8))
        for g in range(8):
            far = levels[np.abs(levels - a[p, g]) >= 10]
            a[p, g + 8] = far[np.random.randint(len(far))]
    return np.exp2(a.ravel()).repeat(32)


def f64(x):
    return np.asarray(x).astype(np.float64)


def striped(idx):
    return np.tile(idx.reshape(-1, 16).T, (8, 1)).astype(np.uint16)


def unstriped(offs):
    return offs[:16].T.reshape(-1).astype(np.int64)


def striped8(idx):
    return np.concatenate([x.reshape(-1, 16).T for x in idx]).astype(np.uint16)


def runs(offs, k):
    lists = np.stack([offs[16 * r : 16 * r + 16].T.reshape(-1) for r in range(8)]).astype(np.int64)
    return lists[np.arange(k) % 512 // 64]


def pack_weight(w):
    k, n = w.shape
    w = f64(np.asarray(w, np.float32).astype(ml_dtypes.bfloat16)).reshape(k // 32, 32, n)
    amax = np.abs(w).max(1)
    byte = np.clip(np.where(amax > 0, np.frexp(amax)[1] - 1 + 127 - 7, 1), 1, 254)
    scaled = (w * np.exp2(127.0 - byte)[:, None, :]).reshape(k, n).astype(np.float32)
    words = np.ascontiguousarray(scaled.reshape(k // 512, 128, 4, n).transpose(0, 1, 3, 2)).astype(ml_dtypes.float8_e4m3fn).view(np.uint8)
    return words, np.ascontiguousarray(byte.astype(np.uint8).reshape(k // 512, 16, n))


def unpack_weight(words, scales):
    g, p, n, _ = words.shape
    vals = np.ascontiguousarray(words).view(ml_dtypes.float8_e4m3fn).astype(np.float64) * np.repeat(np.exp2(scales.astype(np.float64) - 127.0), 8, axis=1)[..., None]
    return vals.transpose(0, 1, 3, 2).reshape(g * 512, n)


K, T, S, H, G, U = 512, 2048, 256, 512, 2048, 512


def setup_inputs():
    n = np.random.standard_normal
    s = mx_kscale(K)[:, None]
    packed_xT = pack_weight(n((K, T)) * s)
    packed_dT = pack_weight(n((K, G)) / s)
    perm = np.random.permutation(U)
    return {
        "x_words": packed_xT[0],
        "x_scales": packed_xT[1],
        "w1": (n((K, H)) / np.sqrt(K) / s).astype(np.float32),
        "gs": (np.random.uniform(0.5, 1.5, (K, 1)) * s).astype(np.float32),
        "d_words": packed_dT[0],
        "d_scales": packed_dT[1],
        "offs": striped8(np.random.randint(0, T, (8, S))),
        "k1": striped8(np.random.randint(0, G, (8, H))),
        "n1": striped(perm[:S]),
        "n2": striped(perm[S:]),
        "n3": striped(np.random.permutation(S)),
    }


def reference(x_words, x_scales, w1, gs, d_words, d_scales, offs, k1, n1, n2, n3):
    d_k1 = unpack_weight(d_words, d_scales)[np.arange(K)[:, None], runs(k1, K)]
    xq = unpack_weight(x_words, x_scales)[np.arange(K)[:, None], runs(offs, K)]
    y = mxq(f64(w1), 0, "e4m3").T @ xq
    z = f64(gs) * y
    h = 0.0625 * ((d_k1.T @ mxq(z, 0, "e4m3")))
    nw = h - h[:, unstriped(n3)]
    ph = np.zeros((H, U))
    ph[:, unstriped(n1)] = h
    out = ph.copy()
    out[:, unstriped(n2)] = nw
    return out

@@ -1,0 +1,182 @@
+from contextlib import ExitStack
+
+import concourse.mybir as mybir
+
+K, T, S, H, G, U = 512, 2048, 256, 512, 2048, 512
+FLOPS = 2 * K * H * S + 2 * K * H * S
+
+F32 = mybir.dt.float32
+BF16 = mybir.dt.bfloat16
+I32 = mybir.dt.int32
+U32 = mybir.dt.uint32
+U16 = mybir.dt.uint16
+U8 = mybir.dt.uint8
+FP8X4 = mybir.dt.float8_e4m3fn_x4
+COPY = mybir.ActivationFunctionType.Copy
+MULT = mybir.AluOpType.mult
+SUBTRACT = mybir.AluOpType.subtract
+
+P = 128
+PACK = 4
+STRIPE = 16
+HALF = S // 2
+SPARE = 16
+
+
+def tile_picked_hdenseipagq_none_p_kernel(
+    tc, x_words, x_scales, w1, gs, d_words, d_scales, offs, k1, n1, n2, n3, out
+):
+    nc = tc.nc
+    blocks = H // P
+    with ExitStack() as ctx:
+        sb = ctx.enter_context(tc.tile_pool(name="sb", bufs=1))
+        ps = ctx.enter_context(tc.psum_pool(name="ps", bufs=1))
+
+        offs_t = sb.tile([P, S // STRIPE], U16, name="offs_t")
+        k1_t = sb.tile([P, H // STRIPE], U16, name="k1_t")
+        n1_t = sb.tile([P, S // STRIPE], U16, name="n1_t")
+        n2_t = sb.tile([P, S // STRIPE], U16, name="n2_t")
+        n3_t = sb.tile([P, S // STRIPE], U16, name="n3_t")
+        xs_win = sb.tile([P, T], U8, name="xs_win")
+        ds_win = sb.tile([P, G], U8, name="ds_win")
+        xw_win = sb.tile([P, T], U32, name="xw_win")
+        dw_win = sb.tile([P, G], U32, name="dw_win")
+        picked_scales = sb.tile([P, S + H], U8, name="picked_scales", align_bytes=64)
+        plane = sb.tile([P, S + H], U8, name="plane", align_bytes=64)
+        gs_t = sb.tile([P, PACK], F32, name="gs_t")
+        w_raw = [sb.tile([P, PACK, H // 2], F32, name="w_raw%d" % c) for c in range(2)]
+        w_bf = sb.tile([P, PACK, P, PACK], BF16, name="w_bf", align_bytes=64)
+        w_codes = sb.tile([P, H], U32, name="w_codes", align_bytes=64)
+        w_scales = sb.tile([P, H], U8, name="w_scales", align_bytes=64)
+        x_codes = sb.tile([P, S], U32, name="x_codes", align_bytes=64)
+        d_codes = sb.tile([P, H], U32, name="d_codes", align_bytes=64)
+        z_bf = [sb.tile([P, HALF, PACK], BF16, name="z_bf%d" % c, align_bytes=64) for c in range(2)]
+        z_codes = sb.tile([P, S], U32, name="z_codes", align_bytes=64)
+        z_scales = sb.tile([P, S], U8, name="z_scales", align_bytes=64)
+        h = [sb.tile([P, S + SPARE], F32, name="h%d" % a) for a in range(blocks)]
+        other = [sb.tile([P, S], F32, name="other%d" % a) for a in range(blocks)]
+        nw = [sb.tile([P, S], F32, name="nw%d" % a) for a in range(blocks)]
+        page = [sb.tile([P, U], F32, name="page%d" % a) for a in range(blocks)]
+
+        nc.vector.memset(xs_win[:].bitcast(I32), 0)
+        nc.vector.memset(ds_win[:].bitcast(I32), 0)
+        nc.vector.memset(plane[:].bitcast(I32), 0)
+
+        nc.sync.dma_start(offs_t[:], offs)
+        nc.sync.dma_start(k1_t[:], k1)
+        nc.scalar.dma_start(out=xs_win[0:P:8, :].bitcast(I32), in_=x_scales[0].bitcast(I32))
+        nc.scalar.dma_start(out=ds_win[0:P:8, :].bitcast(I32), in_=d_scales[0].bitcast(I32))
+        w_rows = w1.rearrange("(p j) c -> p j c", j=PACK)
+        for c in range(2):
+            nc.sync.dma_start(out=w_raw[c][:], in_=w_rows[:, :, c * (H // 2) : (c + 1) * (H // 2)])
+        nc.sync.dma_start(out=xw_win[:].bitcast(I32), in_=x_words[0].rearrange("p n t -> p (n t)").bitcast(I32))
+        nc.sync.dma_start(out=dw_win[:].bitcast(I32), in_=d_words[0].rearrange("p n t -> p (n t)").bitcast(I32))
+        nc.scalar.dma_start(out=gs_t[:], in_=gs.rearrange("(p t) o -> p (t o)", t=PACK))
+        nc.sync.dma_start(n1_t[:], n1)
+        nc.sync.dma_start(n3_t[:], n3)
+        nc.sync.dma_start(n2_t[:], n2)
+
+        for a in range(blocks):
+            nc.vector.memset(page[a][:], 0.0)
+            nc.vector.memset(h[a][:, S:], 0.0)
+
+        nc.vector.tensor_copy(picked_scales[:, :S], xs_win[:].indirect(offs_t[:]))
+        nc.vector.tensor_copy(picked_scales[:, S:], ds_win[:].indirect(k1_t[:]))
+
+        cast = [nc.scalar.copy, nc.vector.tensor_copy]
+        for c in range(2):
+            cast[c](
+                out=w_bf[:, :, c * (P // 2) : (c + 1) * (P // 2), :].rearrange("p t m j -> p m j t"),
+                in_=w_raw[c][:].rearrange("p j (m t) -> p m j t", t=PACK),
+            )
+        for j in range(4):
+            nc.scalar.dma_start(out=plane[j:P:32, :].bitcast(I32), in_=picked_scales[8 * j : P : 32, :].bitcast(I32))
+        nc.vector.quantize_mx(
+            out=w_codes[:].bitcast(FP8X4), scales=w_scales[:], in_=w_bf[:].rearrange("p t m j -> p (t m j)")
+        )
+        nc.vector.tensor_copy(x_codes[:], xw_win[:].indirect(offs_t[:]))
+
+        def first_product(c):
+            cols = slice(c * HALF, (c + 1) * HALF)
+            y = ps.tile([P, PACK, HALF], F32, name="y%d" % c)
+            for t in range(PACK):
+                rows = slice(t * P, (t + 1) * P)
+                nc.tensor.matmul_mx(
+                    out=y[:, t, :],
+                    lhsT=w_codes[:, rows].bitcast(FP8X4),
+                    lhsT_scale=w_scales[:, rows],
+                    rhs=x_codes[:, cols].bitcast(FP8X4),
+                    rhs_scale=plane[:, cols],
+                    start=True,
+                    stop=True,
+                )
+            nc.vector.tensor_tensor(
+                z_bf[c][:],
+                y[:].rearrange("p t n -> p n t"),
+                gs_t[:].unsqueeze(1).to_broadcast([P, HALF, PACK]),
+                MULT,
+            )
+
+        def quantise_z(c):
+            cols = slice(c * HALF, (c + 1) * HALF)
+            nc.vector.quantize_mx(
+                out=z_codes[:, cols].bitcast(FP8X4),
+                scales=z_scales[:, cols],
+                in_=z_bf[c][:].rearrange("p n t -> p (n t)"),
+            )
+
+        def gather_d(c):
+            n = H // 2
+            nc.vector.tensor_copy(
+                d_codes[:, c * n : (c + 1) * n],
+                dw_win[:].indirect(k1_t[:, c * n // STRIPE : (c + 1) * n // STRIPE]),
+            )
+
+        def second_product(a, lo, hi):
+            acc = ps.tile([P, hi - lo], F32, name="acc%d_%d" % (a, lo))
+            nc.tensor.matmul_mx(
+                out=acc[:],
+                lhsT=d_codes[:, a * P : (a + 1) * P].bitcast(FP8X4),
+                lhsT_scale=plane[:, S + a * P : S + (a + 1) * P],
+                rhs=z_codes[:, lo:hi].bitcast(FP8X4),
+                rhs_scale=z_scales[:, lo:hi],
+                start=True,
+                stop=True,
+            )
+            nc.vector.tensor_scalar(h[a][:, lo:hi], acc[:], 0.0625, None, MULT)
+
+        def put_h(a, lo, hi):
+            nc.scalar.activation(page[a][:].indirect(n1_t[:, lo // STRIPE : hi // STRIPE]), h[a][:, lo:hi], COPY)
+
+        def fetch(a):
+            nc.scalar.activation(other[a][:], h[a][:].indirect(n3_t[:]), COPY)
+            nc.vector.tensor_tensor(nw[a][:], h[a][:, :S], other[a][:], SUBTRACT)
+
+        def put_nw(a):
+            nc.scalar.activation(page[a][:].indirect(n2_t[:]), nw[a][:], COPY)
+            nc.sync.dma_start(out=out[a * P : (a + 1) * P, :], in_=page[a][:])
+
+        first_product(0)
+        first_product(1)
+        quantise_z(0)
+        gather_d(0)
+        for a in range(2):
+            second_product(a, 0, HALF)
+            put_h(a, 0, HALF)
+        quantise_z(1)
+        for a in range(2):
+            second_product(a, HALF, S)
+        gather_d(1)
+        for a in range(2):
+            fetch(a)
+            put_h(a, HALF, S)
+        for a in range(2, blocks):
+            second_product(a, 0, S)
+        put_nw(0)
+        fetch(2)
+        put_nw(1)
+        fetch(3)
+        put_h(2, 0, S)
+        put_h(3, 0, S)
+        put_nw(2)
+        put_nw(3)

@@ -37,60 +37,67 @@ def tile_picked_hdenseipagq_none_p_kernel(
         n1_t = sb.tile([P, S // STRIPE], U16, name="n1_t")
         n2_t = sb.tile([P, S // STRIPE], U16, name="n2_t")
         n3_t = sb.tile([P, S // STRIPE], U16, name="n3_t")
-        xs_win = sb.tile([P, T], U8, name="xs_win")
+        xs_win = sb.tile([P, T], U8, name="xs_win", tag="xs_then_d")
         ds_win = sb.tile([P, G], U8, name="ds_win")
         xw_win = sb.tile([P, T], U32, name="xw_win")
-        dw_win = sb.tile([P, G], U32, name="dw_win")
-        picked_scales = sb.tile([P, S + H], U8, name="picked_scales", align_bytes=64)
-        plane = sb.tile([P, S + H], U8, name="plane", align_bytes=64)
+        xs_picked = sb.tile([P, S], U8, name="xs_picked")
+        ds_picked = sb.tile([P, H], U8, name="ds_picked")
+        x_plane = sb.tile([P, S], U8, name="x_plane", align_bytes=64)
+        d_plane = sb.tile([P, H], U8, name="d_plane", align_bytes=64)
         gs_t = sb.tile([P, PACK], F32, name="gs_t")
         w_raw = [sb.tile([P, PACK, H // 2], F32, name="w_raw%d" % c) for c in range(2)]
         w_bf = sb.tile([P, PACK, P, PACK], BF16, name="w_bf", align_bytes=64)
         w_codes = sb.tile([P, H], U32, name="w_codes", align_bytes=64)
         w_scales = sb.tile([P, H], U8, name="w_scales", align_bytes=64)
         x_codes = sb.tile([P, S], U32, name="x_codes", align_bytes=64)
-        d_codes = sb.tile([P, H], U32, name="d_codes", align_bytes=64)
-        z_bf = [sb.tile([P, HALF, PACK], BF16, name="z_bf%d" % c, align_bytes=64) for c in range(2)]
+        d_codes = []
+        z_bf = []
         z_codes = sb.tile([P, S], U32, name="z_codes", align_bytes=64)
         z_scales = sb.tile([P, S], U8, name="z_scales", align_bytes=64)
         h = [sb.tile([P, S + SPARE], F32, name="h%d" % a) for a in range(blocks)]
         other = [sb.tile([P, S], F32, name="other%d" % a) for a in range(blocks)]
-        nw = [sb.tile([P, S], F32, name="nw%d" % a) for a in range(blocks)]
+        nw = []
         page = [sb.tile([P, U], F32, name="page%d" % a) for a in range(blocks)]
 
         nc.vector.memset(xs_win[:].bitcast(I32), 0)
         nc.vector.memset(ds_win[:].bitcast(I32), 0)
-        nc.vector.memset(plane[:].bitcast(I32), 0)
+        nc.vector.memset(x_plane[:].bitcast(I32), 0)
+        nc.vector.memset(d_plane[:].bitcast(I32), 0)
 
         nc.sync.dma_start(offs_t[:], offs)
         nc.sync.dma_start(k1_t[:], k1)
-        nc.scalar.dma_start(out=xs_win[0:P:8, :].bitcast(I32), in_=x_scales[0].bitcast(I32))
-        nc.scalar.dma_start(out=ds_win[0:P:8, :].bitcast(I32), in_=d_scales[0].bitcast(I32))
         w_rows = w1.rearrange("(p j) c -> p j c", j=PACK)
         for c in range(2):
             nc.sync.dma_start(out=w_raw[c][:], in_=w_rows[:, :, c * (H // 2) : (c + 1) * (H // 2)])
-        nc.sync.dma_start(out=xw_win[:].bitcast(I32), in_=x_words[0].rearrange("p n t -> p (n t)").bitcast(I32))
-        nc.sync.dma_start(out=dw_win[:].bitcast(I32), in_=d_words[0].rearrange("p n t -> p (n t)").bitcast(I32))
+            if c == 0:
+                nc.sync.dma_start(out=xs_win[0:P:8, :].bitcast(I32), in_=x_scales[0].bitcast(I32))
+                nc.sync.dma_start(out=ds_win[0:P:8, :].bitcast(I32), in_=d_scales[0].bitcast(I32))
         nc.scalar.dma_start(out=gs_t[:], in_=gs.rearrange("(p t) o -> p (t o)", t=PACK))
         nc.sync.dma_start(n1_t[:], n1)
         nc.sync.dma_start(n3_t[:], n3)
         nc.sync.dma_start(n2_t[:], n2)
+        nc.sync.dma_start(out=xw_win[:].bitcast(I32), in_=x_words[0].rearrange("p n t -> p (n t)").bitcast(I32))
 
         for a in range(blocks):
             nc.vector.memset(page[a][:], 0.0)
             nc.vector.memset(h[a][:, S:], 0.0)
 
-        nc.vector.tensor_copy(picked_scales[:, :S], xs_win[:].indirect(offs_t[:]))
-        nc.vector.tensor_copy(picked_scales[:, S:], ds_win[:].indirect(k1_t[:]))
+        def place_scales(plane, picked):
+            for j in range(4):
+                nc.sync.dma_start(out=plane[j:P:32, :].bitcast(I32), in_=picked[8 * j : P : 32, :].bitcast(I32))
 
-        cast = [nc.scalar.copy, nc.vector.tensor_copy]
-        for c in range(2):
-            cast[c](
-                out=w_bf[:, :, c * (P // 2) : (c + 1) * (P // 2), :].rearrange("p t m j -> p m j t"),
-                in_=w_raw[c][:].rearrange("p j (m t) -> p m j t", t=PACK),
+        nc.vector.tensor_copy(xs_picked[:], xs_win[:].indirect(offs_t[:]))
+        place_scales(x_plane, xs_picked)
+        dw_win = sb.tile([P, G], U32, name="dw_win", tag="xs_then_d")
+        nc.sync.dma_start(out=dw_win[:].bitcast(I32), in_=d_words[0].rearrange("p n t -> p (n t)").bitcast(I32))
+        nc.vector.tensor_copy(ds_picked[:], ds_win[:].indirect(k1_t[:]))
+        place_scales(d_plane, ds_picked)
+
+        for cast, c, lo, hi in ((nc.scalar.copy, 0, 0, 64), (nc.scalar.copy, 1, 0, 32), (nc.vector.tensor_copy, 1, 32, 64)):
+            cast(
+                out=w_bf[:, :, c * (P // 2) + lo : c * (P // 2) + hi, :].rearrange("p t m j -> p m j t"),
+                in_=w_raw[c][:].rearrange("p j (m t) -> p m j t", t=PACK)[:, lo:hi, :, :],
             )
-        for j in range(4):
-            nc.scalar.dma_start(out=plane[j:P:32, :].bitcast(I32), in_=picked_scales[8 * j : P : 32, :].bitcast(I32))
         nc.vector.quantize_mx(
             out=w_codes[:].bitcast(FP8X4), scales=w_scales[:], in_=w_bf[:].rearrange("p t m j -> p (t m j)")
         )
@@ -98,7 +105,7 @@ def tile_picked_hdenseipagq_none_p_kernel(
 
         def first_product(c):
             cols = slice(c * HALF, (c + 1) * HALF)
-            y = ps.tile([P, PACK, HALF], F32, name="y%d" % c)
+            y = ps.tile([P, PACK, HALF], F32, name="y%d" % c, tag="shared%d" % c)
             for t in range(PACK):
                 rows = slice(t * P, (t + 1) * P)
                 nc.tensor.matmul_mx(
@@ -106,10 +113,14 @@ def tile_picked_hdenseipagq_none_p_kernel(
                     lhsT=w_codes[:, rows].bitcast(FP8X4),
                     lhsT_scale=w_scales[:, rows],
                     rhs=x_codes[:, cols].bitcast(FP8X4),
-                    rhs_scale=plane[:, cols],
+                    rhs_scale=x_plane[:, cols],
                     start=True,
                     stop=True,
                 )
+            return y
+
+        def weigh(c, y):
+            z_bf.append(sb.tile([P, HALF, PACK], BF16, name="z_bf%d" % c, tag="half%d" % c, align_bytes=64))
             nc.vector.tensor_tensor(
                 z_bf[c][:],
                 y[:].rearrange("p t n -> p n t"),
@@ -126,57 +137,55 @@ def tile_picked_hdenseipagq_none_p_kernel(
             )
 
         def gather_d(c):
-            n = H // 2
-            nc.vector.tensor_copy(
-                d_codes[:, c * n : (c + 1) * n],
-                dw_win[:].indirect(k1_t[:, c * n // STRIPE : (c + 1) * n // STRIPE]),
-            )
+            d_codes.append(sb.tile([P, H // 2], U32, name="d_codes%d" % c, tag=("d0", "half0")[c], align_bytes=64))
+            nc.vector.tensor_copy(d_codes[c][:], dw_win[:].indirect(k1_t[:, c * (H // 2) // STRIPE : (c + 1) * (H // 2) // STRIPE]))
 
         def second_product(a, lo, hi):
-            acc = ps.tile([P, hi - lo], F32, name="acc%d_%d" % (a, lo))
+            acc = ps.tile([P, hi - lo], F32, name="acc%d_%d" % (a, lo), tag="shared%d" % (1 - lo // HALF) if a == 0 else "acc%d_%d" % (a, lo))
             nc.tensor.matmul_mx(
                 out=acc[:],
-                lhsT=d_codes[:, a * P : (a + 1) * P].bitcast(FP8X4),
-                lhsT_scale=plane[:, S + a * P : S + (a + 1) * P],
+                lhsT=d_codes[a // 2][:, a % 2 * P : (a % 2 + 1) * P].bitcast(FP8X4),
+                lhsT_scale=d_plane[:, a * P : (a + 1) * P],
                 rhs=z_codes[:, lo:hi].bitcast(FP8X4),
                 rhs_scale=z_scales[:, lo:hi],
                 start=True,
                 stop=True,
             )
-            nc.vector.tensor_scalar(h[a][:, lo:hi], acc[:], 0.0625, None, MULT)
+            if (a, lo) == (0, 0):
+                nc.scalar.activation(h[a][:, lo:hi], acc[:], COPY, scale=0.0625)
+            else:
+                nc.vector.tensor_scalar(h[a][:, lo:hi], acc[:], 0.0625, None, MULT)
 
         def put_h(a, lo, hi):
             nc.scalar.activation(page[a][:].indirect(n1_t[:, lo // STRIPE : hi // STRIPE]), h[a][:, lo:hi], COPY)
 
         def fetch(a):
             nc.scalar.activation(other[a][:], h[a][:].indirect(n3_t[:]), COPY)
+            nw.append(sb.tile([P, S], F32, name="nw%d" % a, tag="half0" if a == 0 else "nw%d" % a, align_bytes=64))
             nc.vector.tensor_tensor(nw[a][:], h[a][:, :S], other[a][:], SUBTRACT)
 
         def put_nw(a):
             nc.scalar.activation(page[a][:].indirect(n2_t[:]), nw[a][:], COPY)
             nc.sync.dma_start(out=out[a * P : (a + 1) * P, :], in_=page[a][:])
 
-        first_product(0)
-        first_product(1)
+        weigh(0, first_product(0))
         quantise_z(0)
         gather_d(0)
         for a in range(2):
             second_product(a, 0, HALF)
             put_h(a, 0, HALF)
-        quantise_z(1)
-        for a in range(2):
-            second_product(a, HALF, S)
+        y = first_product(1)
         gather_d(1)
-        for a in range(2):
+        weigh(1, y)
+        for a in range(2, blocks):
+            second_product(a, 0, HALF)
+            put_h(a, 0, HALF)
+        quantise_z(1)
+        for a in range(blocks):
+            second_product(a, HALF, S)
+        for a in range(blocks):
             fetch(a)
             put_h(a, HALF, S)
-        for a in range(2, blocks):
-            second_product(a, 0, S)
-        put_nw(0)
-        fetch(2)
-        put_nw(1)
-        fetch(3)
-        put_h(2, 0, S)
-        put_h(3, 0, S)
-        put_nw(2)
-        put_nw(3)
+            if a > 0:
+                put_nw(a - 1)
+        put_nw(blocks - 1)

@@ -41,7 +41,7 @@ def tile_picked_hdenseipagq_none_p_kernel(
         ds_win = sb.tile([P, G], U8, name="ds_win")
         xw_win = sb.tile([P, T], U32, name="xw_win")
         xs_picked = sb.tile([P, S], U8, name="xs_picked")
-        ds_picked = sb.tile([P, H], U8, name="ds_picked")
+        ds_picked = sb.tile([P, H], U8, name="ds_picked", tag="ds_then_z", align_bytes=64)
         x_plane = sb.tile([P, S], U8, name="x_plane", align_bytes=64)
         d_plane = sb.tile([P, H], U8, name="d_plane", align_bytes=64)
         gs_t = sb.tile([P, PACK], F32, name="gs_t")
@@ -53,7 +53,6 @@ def tile_picked_hdenseipagq_none_p_kernel(
         d_codes = []
         z_bf = []
         z_codes = sb.tile([P, S], U32, name="z_codes", align_bytes=64)
-        z_scales = sb.tile([P, S], U8, name="z_scales", align_bytes=64)
         h = [sb.tile([P, S + SPARE], F32, name="h%d" % a) for a in range(blocks)]
         other = [sb.tile([P, S], F32, name="other%d" % a) for a in range(blocks)]
         nw = []
@@ -75,8 +74,8 @@ def tile_picked_hdenseipagq_none_p_kernel(
         nc.scalar.dma_start(out=gs_t[:], in_=gs.rearrange("(p t) o -> p (t o)", t=PACK))
         nc.sync.dma_start(n1_t[:], n1)
         nc.sync.dma_start(n3_t[:], n3)
-        nc.sync.dma_start(n2_t[:], n2)
         nc.sync.dma_start(out=xw_win[:].bitcast(I32), in_=x_words[0].rearrange("p n t -> p (n t)").bitcast(I32))
+        nc.sync.dma_start(n2_t[:], n2)
 
         for a in range(blocks):
             nc.vector.memset(page[a][:], 0.0)
@@ -95,13 +94,15 @@ def tile_picked_hdenseipagq_none_p_kernel(
 
         for cast, c, lo, hi in ((nc.scalar.copy, 0, 0, 64), (nc.scalar.copy, 1, 0, 32), (nc.vector.tensor_copy, 1, 32, 64)):
             cast(
-                out=w_bf[:, :, c * (P // 2) + lo : c * (P // 2) + hi, :].rearrange("p t m j -> p m j t"),
-                in_=w_raw[c][:].rearrange("p j (m t) -> p m j t", t=PACK)[:, lo:hi, :, :],
+                out=w_bf[:, :, c * (P // 2) + lo : c * (P // 2) + hi, :].rearrange("p t m j -> p m t j"),
+                in_=w_raw[c][:].rearrange("p j (m t) -> p m t j", t=PACK)[:, lo:hi, :, :],
             )
         nc.vector.quantize_mx(
             out=w_codes[:].bitcast(FP8X4), scales=w_scales[:], in_=w_bf[:].rearrange("p t m j -> p (t m j)")
         )
         nc.vector.tensor_copy(x_codes[:], xw_win[:].indirect(offs_t[:]))
+
+        z_scales = sb.tile([P, S], U8, name="z_scales", tag="ds_then_z", align_bytes=64)
 
         def first_product(c):
             cols = slice(c * HALF, (c + 1) * HALF)

from contextlib import ExitStack

import concourse.mybir as mybir

K, T, S, H, G, U = 512, 2048, 256, 512, 2048, 512
FLOPS = 2 * K * H * S + 2 * K * H * S

F32 = mybir.dt.float32
BF16 = mybir.dt.bfloat16
I32 = mybir.dt.int32
U32 = mybir.dt.uint32
U16 = mybir.dt.uint16
U8 = mybir.dt.uint8
FP8X4 = mybir.dt.float8_e4m3fn_x4
COPY = mybir.ActivationFunctionType.Copy
MULT = mybir.AluOpType.mult
SUBTRACT = mybir.AluOpType.subtract

P = 128
PACK = 4
STRIPE = 16
HALF = S // 2
SPARE = 16


def tile_picked_hdenseipagq_none_p_kernel(
    tc, x_words, x_scales, w1, gs, d_words, d_scales, offs, k1, n1, n2, n3, out
):
    nc = tc.nc
    blocks = H // P
    with ExitStack() as ctx:
        sb = ctx.enter_context(tc.tile_pool(name="sb", bufs=1))
        ps = ctx.enter_context(tc.psum_pool(name="ps", bufs=1))

        offs_t = sb.tile([P, S // STRIPE], U16, name="offs_t")
        k1_t = sb.tile([P, H // STRIPE], U16, name="k1_t")
        n1_t = sb.tile([P, S // STRIPE], U16, name="n1_t")
        n2_t = sb.tile([P, S // STRIPE], U16, name="n2_t")
        n3_t = sb.tile([P, S // STRIPE], U16, name="n3_t")
        xs_win = sb.tile([P, T], U8, name="xs_win", tag="xs_then_d")
        ds_win = sb.tile([P, G], U8, name="ds_win")
        xw_win = sb.tile([P, T], U32, name="xw_win")
        xs_picked = sb.tile([P, S], U8, name="xs_picked")
        ds_picked = sb.tile([P, H], U8, name="ds_picked", tag="ds_then_z", align_bytes=64)
        x_plane = sb.tile([P, S], U8, name="x_plane", align_bytes=64)
        d_plane = sb.tile([P, H], U8, name="d_plane", align_bytes=64)
        gs_t = sb.tile([P, PACK], F32, name="gs_t")
        w_raw = [sb.tile([P, PACK, H // 2], F32, name="w_raw%d" % c) for c in range(2)]
        w_bf = sb.tile([P, PACK, P, PACK], BF16, name="w_bf", align_bytes=64)
        w_codes = sb.tile([P, H], U32, name="w_codes", align_bytes=64)
        w_scales = sb.tile([P, H], U8, name="w_scales", align_bytes=64)
        x_codes = sb.tile([P, S], U32, name="x_codes", align_bytes=64)
        d_codes = []
        z_bf = []
        z_codes = sb.tile([P, S], U32, name="z_codes", align_bytes=64)
        h = [sb.tile([P, S + SPARE], F32, name="h%d" % a) for a in range(blocks)]
        other = [sb.tile([P, S], F32, name="other%d" % a) for a in range(blocks)]
        nw = []
        page = [sb.tile([P, U], F32, name="page%d" % a) for a in range(blocks)]

        nc.vector.memset(xs_win[:].bitcast(I32), 0)
        nc.vector.memset(ds_win[:].bitcast(I32), 0)
        nc.vector.memset(x_plane[:].bitcast(I32), 0)
        nc.vector.memset(d_plane[:].bitcast(I32), 0)

        nc.sync.dma_start(offs_t[:], offs)
        nc.sync.dma_start(k1_t[:], k1)
        w_rows = w1.rearrange("(p j) c -> p j c", j=PACK)
        for c in range(2):
            nc.sync.dma_start(out=w_raw[c][:], in_=w_rows[:, :, c * (H // 2) : (c + 1) * (H // 2)])
            if c == 0:
                nc.sync.dma_start(out=xs_win[0:P:8, :].bitcast(I32), in_=x_scales[0].bitcast(I32))
                nc.sync.dma_start(out=ds_win[0:P:8, :].bitcast(I32), in_=d_scales[0].bitcast(I32))
        nc.scalar.dma_start(out=gs_t[:], in_=gs.rearrange("(p t) o -> p (t o)", t=PACK))
        nc.sync.dma_start(n1_t[:], n1)
        nc.sync.dma_start(n3_t[:], n3)
        nc.sync.dma_start(out=xw_win[:].bitcast(I32), in_=x_words[0].rearrange("p n t -> p (n t)").bitcast(I32))
        nc.sync.dma_start(n2_t[:], n2)

        for a in range(blocks):
            nc.vector.memset(page[a][:], 0.0)
            nc.vector.memset(h[a][:, S:], 0.0)

        def place_scales(plane, picked):
            for j in range(4):
                nc.sync.dma_start(out=plane[j:P:32, :].bitcast(I32), in_=picked[8 * j : P : 32, :].bitcast(I32))

        nc.vector.tensor_copy(xs_picked[:], xs_win[:].indirect(offs_t[:]))
        place_scales(x_plane, xs_picked)
        dw_win = sb.tile([P, G], U32, name="dw_win", tag="xs_then_d")
        nc.sync.dma_start(out=dw_win[:].bitcast(I32), in_=d_words[0].rearrange("p n t -> p (n t)").bitcast(I32))
        nc.vector.tensor_copy(ds_picked[:], ds_win[:].indirect(k1_t[:]))
        place_scales(d_plane, ds_picked)

        for cast, c, lo, hi in ((nc.scalar.copy, 0, 0, 64), (nc.scalar.copy, 1, 0, 32), (nc.vector.tensor_copy, 1, 32, 64)):
            cast(
                out=w_bf[:, :, c * (P // 2) + lo : c * (P // 2) + hi, :].rearrange("p t m j -> p m t j"),
                in_=w_raw[c][:].rearrange("p j (m t) -> p m t j", t=PACK)[:, lo:hi, :, :],
            )
        nc.vector.quantize_mx(
            out=w_codes[:].bitcast(FP8X4), scales=w_scales[:], in_=w_bf[:].rearrange("p t m j -> p (t m j)")
        )
        nc.vector.tensor_copy(x_codes[:], xw_win[:].indirect(offs_t[:]))

        z_scales = sb.tile([P, S], U8, name="z_scales", tag="ds_then_z", align_bytes=64)

        def first_product(c):
            cols = slice(c * HALF, (c + 1) * HALF)
            y = ps.tile([P, PACK, HALF], F32, name="y%d" % c, tag="shared%d" % c)
            for t in range(PACK):
                rows = slice(t * P, (t + 1) * P)
                nc.tensor.matmul_mx(
                    out=y[:, t, :],
                    lhsT=w_codes[:, rows].bitcast(FP8X4),
                    lhsT_scale=w_scales[:, rows],
                    rhs=x_codes[:, cols].bitcast(FP8X4),
                    rhs_scale=x_plane[:, cols],
                    start=True,
                    stop=True,
                )
            return y

        def weigh(c, y):
            z_bf.append(sb.tile([P, HALF, PACK], BF16, name="z_bf%d" % c, tag="half%d" % c, align_bytes=64))
            nc.vector.tensor_tensor(
                z_bf[c][:],
                y[:].rearrange("p t n -> p n t"),
                gs_t[:].unsqueeze(1).to_broadcast([P, HALF, PACK]),
                MULT,
            )

        def quantise_z(c):
            cols = slice(c * HALF, (c + 1) * HALF)
            nc.vector.quantize_mx(
                out=z_codes[:, cols].bitcast(FP8X4),
                scales=z_scales[:, cols],
                in_=z_bf[c][:].rearrange("p n t -> p (n t)"),
            )

        def gather_d(c):
            d_codes.append(sb.tile([P, H // 2], U32, name="d_codes%d" % c, tag=("d0", "half0")[c], align_bytes=64))
            nc.vector.tensor_copy(d_codes[c][:], dw_win[:].indirect(k1_t[:, c * (H // 2) // STRIPE : (c + 1) * (H // 2) // STRIPE]))

        def second_product(a, lo, hi):
            acc = ps.tile([P, hi - lo], F32, name="acc%d_%d" % (a, lo), tag="shared%d" % (1 - lo // HALF) if a == 0 else "acc%d_%d" % (a, lo))
            nc.tensor.matmul_mx(
                out=acc[:],
                lhsT=d_codes[a // 2][:, a % 2 * P : (a % 2 + 1) * P].bitcast(FP8X4),
                lhsT_scale=d_plane[:, a * P : (a + 1) * P],
                rhs=z_codes[:, lo:hi].bitcast(FP8X4),
                rhs_scale=z_scales[:, lo:hi],
                start=True,
                stop=True,
            )
            if (a, lo) == (0, 0):
                nc.scalar.activation(h[a][:, lo:hi], acc[:], COPY, scale=0.0625)
            else:
                nc.vector.tensor_scalar(h[a][:, lo:hi], acc[:], 0.0625, None, MULT)

        def put_h(a, lo, hi):
            nc.scalar.activation(page[a][:].indirect(n1_t[:, lo // STRIPE : hi // STRIPE]), h[a][:, lo:hi], COPY)

        def fetch(a):
            nc.scalar.activation(other[a][:], h[a][:].indirect(n3_t[:]), COPY)
            nw.append(sb.tile([P, S], F32, name="nw%d" % a, tag="half0" if a == 0 else "nw%d" % a, align_bytes=64))
            nc.vector.tensor_tensor(nw[a][:], h[a][:, :S], other[a][:], SUBTRACT)

        def put_nw(a):
            nc.scalar.activation(page[a][:].indirect(n2_t[:]), nw[a][:], COPY)
            nc.sync.dma_start(out=out[a * P : (a + 1) * P, :], in_=page[a][:])

        weigh(0, first_product(0))
        quantise_z(0)
        gather_d(0)
        for a in range(2):
            second_product(a, 0, HALF)
            put_h(a, 0, HALF)
        y = first_product(1)
        gather_d(1)
        weigh(1, y)
        for a in range(2, blocks):
            second_product(a, 0, HALF)
            put_h(a, 0, HALF)
        quantise_z(1)
        for a in range(blocks):
            second_product(a, HALF, S)
        for a in range(blocks):
            fetch(a)
            put_h(a, HALF, S)
            if a > 0:
                put_nw(a - 1)
        put_nw(blocks - 1)
